import numpy as np
import ml_dtypes


def mxq(x, axis, fmt="e4m3"):
    dtype, down = {"e4m3": (ml_dtypes.float8_e4m3fn, 7), "e5m2": (ml_dtypes.float8_e5m2, 14)}[fmt]
    v = np.moveaxis(np.asarray(x, np.float32).astype(ml_dtypes.bfloat16).astype(np.float64), axis, -1)
    blocks = v.reshape(v.shape[:-1] + (-1, 32))
    amax = np.abs(blocks).max(-1, keepdims=True)
    byte = np.maximum(np.where(amax > 0, np.frexp(amax)[1] - 1 + 127, 0) - down, 1)
    scale = np.exp2(byte - 127.0)
    codes = (blocks / scale).astype(np.float32).astype(dtype).astype(np.float64)
    return np.moveaxis((codes * scale).reshape(v.shape), -1, axis)


WIDE = False


def mx_kscale(k, group=512):
    if not WIDE:
        return np.ones(k)
    levels = np.array([18, -18])
    if group != 512:
        return np.exp2(np.random.permutation(np.resize(levels, k // group))).repeat(group)
    if k % 512:
        return np.exp2(np.random.permutation(np.resize(levels, k // 32))).repeat(32)
    a = np.empty((k // 512, 16))
    for p in range(k // 512):
        a[p, :8] = np.random.permutation(np.resize(levels, 8))
        for g in range(8):
            far = levels[np.abs(levels - a[p, g]) >= 10]
            a[p, g + 8] = far[np.random.randint(len(far))]
    return np.exp2(a.ravel()).repeat(32)


def f64(x):
    return np.asarray(x).astype(np.float64)


H, D, N = 4, 128, 1024


def setup_inputs():
    n = np.random.standard_normal
    s = mx_kscale(D, 0)
    u = mx_kscale(N)
    t = np.random.uniform(0.5, 2.0, N) * u
    v = n((H, N, 128))
    return {
        "q": n((H, D, N)).astype(np.float32),
        "qa": (np.random.uniform(0.5, 2.0, D) * s)[:, None].astype(np.float32),
        "ka": np.tile(np.random.uniform(0.5, 2.0, D) / s, (128, 1)).astype(np.float32),
        "k": n((H, N, D)).astype(np.float32),
        "t": t.reshape(N, 1).astype(np.float32),
        "v": (v / t[:, None]).astype(np.float32),
        "og": n((H, N, 128)).astype(np.float32),
    }


def reference(q, qa, ka, k, t, v, og):
    fq = (np.square(f64(q)) + 0.125) * f64(qa)
    fk = (np.square(f64(k)) + 0.125) * f64(t) * f64(ka)[:1]
    S = (mxq(fk, 1, "e4m3").transpose(0, 2, 1) @ mxq(f64(v), 1, "e4m3")) / N
    y = mxq(fq, 1, "e4m3").transpose(0, 2, 1) @ mxq(S, 1, "e4m3")
    y = y / (1.0 + np.exp(-f64(og)))
    return y

@@ -1,0 +1,308 @@
+from contextlib import ExitStack
+
+import concourse.mybir as mybir
+
+H, D, N = 4, 128, 1024
+FLOPS = 2 * 2 * H * N * D * 128
+
+F32 = mybir.dt.float32
+BF16 = mybir.dt.bfloat16
+U32 = mybir.dt.uint32
+U8 = mybir.dt.uint8
+FP8X4 = mybir.dt.float8_e4m3fn_x4
+ACT = mybir.ActivationFunctionType
+ALU = mybir.AluOpType
+
+P = 128
+PACK = 4
+ROWS = 32
+PASSES = 2
+PHI_BIAS = 0.125
+QW = 512
+
+
+def tile_rows_lin_sq_gate_kernel(tc, q, qa, ka, k, t, v, og, out):
+    nc = tc.nc
+    k_rows = k.rearrange("h (g p j) d -> h p g (j d)", g=PASSES, j=PACK)
+    v_rows = v.rearrange("h (g p j) e -> h p g (j e)", g=PASSES, j=PACK)
+    q_rows = q.rearrange("h (p j) n -> (h p) j n", j=PACK)
+    og_rows = og.rearrange("h (p s) e -> h p (s e)", s=8)
+    out_rows = out.rearrange("h (p s) e -> h p (s e)", s=8)
+
+    with ExitStack() as ctx:
+        sb = ctx.enter_context(tc.tile_pool(name="sb", bufs=1))
+        ps = ctx.enter_context(tc.psum_pool(name="ps", bufs=1))
+        ctx.enter_context(tc.manual_schedule())
+
+        def tile(name, shape, dtype):
+            return sb.tile(shape, dtype, name=name, align_bytes=64)
+
+        ka_sb = tile("ka_sb", [P, D], F32)
+        t_sb = tile("t_sb", [P, PASSES, PACK], F32)
+        qa_sb = tile("qa_sb", [P, PACK], F32)
+        qa_rep = tile("qa_rep", [P, QW // 8, PACK], F32)
+        k_raw = {}
+        v_raw = {}
+        q_raw = {}
+        og_raw = {}
+
+        def load_k(h, split):
+            if split:
+                for g in range(PASSES):
+                    raw = tile("k_raw%d%d" % (h, g), [P, 512], F32)
+                    nc.sync.dma_start(out=raw[:], in_=k_rows[h, :, g, :])
+                    k_raw[h, g] = raw[:]
+            else:
+                raw = tile("k_raw%d" % h, [P, PASSES, 512], F32)
+                nc.sync.dma_start(out=raw[:], in_=k_rows[h])
+                for g in range(PASSES):
+                    k_raw[h, g] = raw[:, g, :]
+
+        def load_v(h):
+            raw = tile("v_raw%d" % h, [P, PASSES, 512], F32)
+            nc.sync.dma_start(out=raw[:], in_=v_rows[h])
+            v_raw[h] = raw
+
+        def load_q(c):
+            raw = tile("q_raw%d" % c, [P, PACK, QW], F32)
+            nc.sync.dma_start(out=raw[:], in_=q_rows[:, :, c * QW : (c + 1) * QW])
+            q_raw[c] = raw
+
+        def load_og(queue, h, lo, hi):
+            raw = tile("og_raw%d_%d" % (h, lo), [P, hi - lo], F32)
+            queue.dma_start(out=raw[:], in_=og_rows[h, :, lo:hi])
+            og_raw[h, lo] = raw
+
+        tka = [tile("tka%d" % g, [P, 512], F32) for g in range(PASSES)]
+        k_sq = {}
+        fk = [tile("fk%d" % g, [P, PACK, H, 128], BF16) for g in range(PASSES)]
+        fk_codes = [tile("fk_codes%d" % g, [P, 512], U32) for g in range(PASSES)]
+        fk_scales = [tile("fk_scales%d" % g, [P, 512], U8) for g in range(PASSES)]
+        v_bf = [tile("v_bf%d" % h, [P, PASSES, 128, PACK], BF16) for h in range(H)]
+        v_codes = [tile("v_codes%d" % h, [P, 256], U32) for h in range(H)]
+        v_scales = [tile("v_scales%d" % h, [P, 256], U8) for h in range(H)]
+        q_sq = {}
+        fq = [tile("fq%d" % u, [P, 4, 128, PACK], BF16) for u in range(2)]
+        fq_codes = [tile("fq_codes%d" % u, [P, 512], U32) for u in range(2)]
+        fq_scales = [tile("fq_scales%d" % u, [P, 512], U8) for u in range(2)]
+        state_bf = tile("state_bf", [P, 128, PACK], BF16)
+        state_codes = [tile("state_codes%d" % h, [P, 128], U32) for h in range(H)]
+        state_scales = [tile("state_scales%d" % h, [P, 128], U8) for h in range(H)]
+        gate = {(h, u): tile("gate%d%d" % (h, u), [P, 512], F32) for h in range(H) for u in range(2)}
+        result = [tile("result%d" % h, [P, 1024], F32) for h in range(H)]
+        state_bank = [ps.tile([P, PACK, 128], F32, name="state_bank%d" % i) for i in range(2)]
+        y_banks = [ps.tile([P, 512], F32, name="y_bank%d" % i) for i in range(6)]
+        y_bank = {(0, 0): y_banks[0], (0, 1): y_banks[0], (1, 0): y_banks[1], (1, 1): y_banks[1],
+                  (2, 0): y_banks[2], (2, 1): y_banks[3], (3, 0): y_banks[4], (3, 1): y_banks[5]}
+
+        def make_tka(g):
+            shape = [P, PACK, ROWS, PACK]
+            nc.vector.tensor_tensor(
+                out=tka[g][:].rearrange("p (x m j) -> p x m j", x=PACK, j=PACK),
+                in0=ka_sb[:].rearrange("p (m x) -> p x m", x=PACK).unsqueeze(3).to_broadcast(shape),
+                in1=t_sb[:, g, :].unsqueeze(1).unsqueeze(1).to_broadcast(shape),
+                op=ALU.mult,
+            )
+
+        def square_k(h, g):
+            sq = tile("k_sq%d%d" % (h, g), [P, 512], F32)
+            nc.scalar.activation(
+                out=sq[:].rearrange("p (x m j) -> p m j x", x=PACK, j=PACK),
+                in_=k_raw[h, g].rearrange("p (j m x) -> p m j x", j=PACK, x=PACK),
+                func=ACT.Square,
+            )
+            k_sq[h, g] = sq
+
+        def weigh_k(h, g):
+            nc.vector.scalar_tensor_tensor(
+                out=fk[g][:, :, h, :],
+                in0=k_sq[h, g][:].rearrange("p (x w) -> p x w", x=PACK),
+                scalar=PHI_BIAS,
+                in1=tka[g][:].rearrange("p (x w) -> p x w", x=PACK),
+                op0=ALU.add,
+                op1=ALU.mult,
+            )
+
+        def quantize(codes, scales, values):
+            nc.vector.quantize_mx(out=codes.bitcast(FP8X4), scales=scales, in_=values)
+
+        def quantize_k(g):
+            quantize(fk_codes[g][:], fk_scales[g][:], fk[g][:].rearrange("p x h w -> p (x h w)"))
+
+        def round_v(h, on_scalar):
+            dst = v_bf[h][:].rearrange("p g (c i) j -> p g c j i", i=4)
+            src = v_raw[h][:].rearrange("p g (j c i) -> p g c j i", j=PACK, i=4)
+            if on_scalar:
+                nc.scalar.copy(out=dst, in_=src)
+            else:
+                nc.vector.tensor_copy(out=dst, in_=src)
+
+        def quantize_v(h):
+            quantize(v_codes[h][:], v_scales[h][:], v_bf[h][:].rearrange("p g e j -> p (g e j)"))
+
+        def state_matmuls(h):
+            for x in range(PACK):
+                cols = slice(128 * x, 128 * (x + 1))
+                for g in range(PASSES):
+                    vcols = slice(128 * g, 128 * (g + 1))
+                    nc.tensor.matmul_mx(
+                        out=state_bank[h % 2][:, x, :],
+                        lhsT=fk_codes[g][:, cols].bitcast(FP8X4),
+                        lhsT_scale=fk_scales[g][:, cols],
+                        rhs=v_codes[h][:, vcols].bitcast(FP8X4),
+                        rhs_scale=v_scales[h][:, vcols],
+                        start=(g == 0),
+                        stop=(g == PASSES - 1),
+                    )
+
+        def round_state(h):
+            rows = slice(ROWS * h, ROWS * (h + 1))
+            nc.scalar.activation(
+                out=state_bf[rows],
+                in_=state_bank[h % 2][rows].rearrange("p x e -> p e x"),
+                func=ACT.Copy,
+                scale=1.0 / N,
+            )
+
+        def quantize_state(h):
+            rows = slice(0, ROWS * (h + 1))
+            quantize(state_codes[h][rows], state_scales[h][rows], state_bf[rows].rearrange("p e x -> p (e x)"))
+
+        def square_q(c, u):
+            sq = tile("q_sq%d%d" % (c, u), [P, 4, QW // 8, PACK], F32)
+            nc.scalar.activation(
+                out=sq[:].rearrange("p r m j -> p m j r"),
+                in_=q_raw[c][:].rearrange("p j (m u r) -> p u m j r", u=2, r=4)[:, u],
+                func=ACT.Square,
+            )
+            q_sq[c, u] = sq
+
+        def weigh_q(c, u):
+            m = QW // 8
+            nc.vector.scalar_tensor_tensor(
+                out=fq[u][:].rearrange("p r m j -> p r (m j)")[:, :, c * m * PACK : (c + 1) * m * PACK],
+                in0=q_sq[c, u][:].rearrange("p r m j -> p r (m j)"),
+                scalar=PHI_BIAS,
+                in1=qa_rep[:].rearrange("p m j -> p (m j)").unsqueeze(1).to_broadcast([P, 4, m * PACK]),
+                op0=ALU.add,
+                op1=ALU.mult,
+            )
+
+        def quantize_q(u):
+            quantize(fq_codes[u][:], fq_scales[u][:], fq[u][:].rearrange("p r m j -> p (r m j)"))
+
+        def read_matmuls(h, u):
+            rows = slice(ROWS * h, ROWS * (h + 1))
+            for r in range(4):
+                cols = slice(128 * r, 128 * (r + 1))
+                nc.tensor.matmul_mx(
+                    out=y_bank[h, u][:, cols],
+                    lhsT=fq_codes[u][rows, cols].bitcast(FP8X4),
+                    lhsT_scale=fq_scales[u][rows, cols],
+                    rhs=state_codes[h][rows].bitcast(FP8X4),
+                    rhs_scale=state_scales[h][rows],
+                    start=True,
+                    stop=True,
+                )
+
+        def sigmoid(h, lo, hi, base):
+            u = lo // 512
+            nc.scalar.activation(
+                out=gate[h, u][:, lo - 512 * u : hi - 512 * u],
+                in_=og_raw[h, base][:, lo - base : hi - base],
+                func=ACT.Sigmoid,
+            )
+
+        def apply_gate(h, u):
+            nc.vector.tensor_tensor(
+                out=result[h][:, 512 * u : 512 * (u + 1)], in0=y_bank[h, u][:], in1=gate[h, u][:], op=ALU.mult
+            )
+
+        def store(h, lo, hi):
+            nc.sync.dma_start(out=out_rows[h, :, lo:hi], in_=result[h][:, lo:hi])
+
+
+        load_k(0, True)
+        nc.scalar.dma_start(out=ka_sb[:], in_=ka)
+        nc.scalar.dma_start(out=t_sb[:], in_=t.rearrange("(g p j) o -> p g (j o)", g=PASSES, j=PACK))
+        load_og(nc.scalar, 0, 0, 128)
+        for h in range(1, H):
+            load_k(h, False)
+        nc.sync.dma_start(
+            out=qa_sb[:], in_=qa.rearrange("(p j) o -> p (j o)", j=PACK).unsqueeze(0).to_broadcast([H, ROWS, PACK])
+        )
+        load_v(0)
+        load_q(0)
+        load_v(1)
+        load_v(2)
+        load_q(1)
+        load_v(3)
+        load_og(nc.sync, 0, 128, 1024)
+        load_og(nc.sync, 1, 0, 1024)
+        load_og(nc.sync, 2, 0, 1024)
+        load_og(nc.sync, 3, 0, 512)
+        load_og(nc.sync, 3, 512, 1024)
+
+        sigmoid(0, 0, 128, 0)
+        for g in range(PASSES):
+            make_tka(g)
+        for h in range(H):
+            for g in range(PASSES):
+                square_k(h, g)
+                weigh_k(h, g)
+        round_v(0, True)
+        nc.vector.tensor_copy(out=qa_rep[:], in_=qa_sb[:].unsqueeze(1).to_broadcast([P, QW // 8, PACK]))
+        quantize_k(0)
+        quantize_k(1)
+        quantize_v(0)
+        state_matmuls(0)
+        square_q(0, 0)
+        square_q(0, 1)
+        round_v(1, False)
+        weigh_q(0, 0)
+        quantize_v(1)
+        state_matmuls(1)
+        round_state(0)
+        round_v(2, True)
+        weigh_q(0, 1)
+        quantize_state(0)
+        quantize_v(2)
+        state_matmuls(2)
+        round_state(1)
+        quantize_state(1)
+        square_q(1, 0)
+        square_q(1, 1)
+        round_v(3, False)
+        weigh_q(1, 0)
+        quantize_v(3)
+        state_matmuls(3)
+        quantize_q(0)
+        read_matmuls(0, 0)
+        read_matmuls(1, 0)
+        round_state(2)
+        weigh_q(1, 1)
+        quantize_state(2)
+        quantize_q(1)
+        sigmoid(0, 128, 512, 128)
+        sigmoid(1, 0, 512, 0)
+        round_state(3)
+        sigmoid(0, 512, 1024, 128)
+        sigmoid(1, 512, 1024, 0)
+        read_matmuls(2, 0)
+        read_matmuls(2, 1)
+        apply_gate(0, 0)
+        read_matmuls(0, 1)
+        apply_gate(1, 0)
+        read_matmuls(1, 1)
+        quantize_state(3)
+        read_matmuls(3, 0)
+        read_matmuls(3, 1)
+        apply_gate(0, 1)
+        store(0, 0, 1024)
+        apply_gate(1, 1)
+        store(1, 0, 1024)
+        for h in (2, 3):
+            for u in range(2):
+                sigmoid(h, 512 * u, 512 * (u + 1), 512 * u if h == 3 else 0)
+                apply_gate(h, u)
+                store(h, 512 * u, 512 * (u + 1))

@@ -3,7 +3,7 @@ from contextlib import ExitStack
 import concourse.mybir as mybir
 
 H, D, N = 4, 128, 1024
-FLOPS = 2 * 2 * H * N * D * 128
+FLOPS = 2 * 2 * H * N * D * D
 
 F32 = mybir.dt.float32
 BF16 = mybir.dt.bfloat16
@@ -15,10 +15,15 @@ ALU = mybir.AluOpType
 
 P = 128
 PACK = 4
-ROWS = 32
-PASSES = 2
+ROWS = D // PACK
+PASSES = N // (P * PACK)
+BANK = 512
+HALVES = 2
 PHI_BIAS = 0.125
-QW = 512
+Q_LOADS = 2
+Q_PIECES = 4
+Q_M = P // Q_PIECES
+FIRST_GATE = D
 
 
 def tile_rows_lin_sq_gate_kernel(tc, q, qa, ka, k, t, v, og, out):
@@ -26,131 +31,144 @@ def tile_rows_lin_sq_gate_kernel(tc, q, qa, ka, k, t, v, og, out):
     k_rows = k.rearrange("h (g p j) d -> h p g (j d)", g=PASSES, j=PACK)
     v_rows = v.rearrange("h (g p j) e -> h p g (j e)", g=PASSES, j=PACK)
     q_rows = q.rearrange("h (p j) n -> (h p) j n", j=PACK)
-    og_rows = og.rearrange("h (p s) e -> h p (s e)", s=8)
-    out_rows = out.rearrange("h (p s) e -> h p (s e)", s=8)
+    og_rows = og.rearrange("h (m s) e -> h m (s e)", m=P)
+    out_rows = out.rearrange("h (m s) e -> h m (s e)", m=P)
 
     with ExitStack() as ctx:
-        sb = ctx.enter_context(tc.tile_pool(name="sb", bufs=1))
-        ps = ctx.enter_context(tc.psum_pool(name="ps", bufs=1))
+        sbuf = ctx.enter_context(tc.tile_pool(name="sbuf", bufs=1))
+        psum = ctx.enter_context(tc.psum_pool(name="psum", bufs=1))
         ctx.enter_context(tc.manual_schedule())
 
         def tile(name, shape, dtype):
-            return sb.tile(shape, dtype, name=name, align_bytes=64)
+            return sbuf.tile(shape, dtype, name=name, align_bytes=64)
 
-        ka_sb = tile("ka_sb", [P, D], F32)
-        t_sb = tile("t_sb", [P, PASSES, PACK], F32)
-        qa_sb = tile("qa_sb", [P, PACK], F32)
-        qa_rep = tile("qa_rep", [P, QW // 8, PACK], F32)
-        k_raw = {}
-        v_raw = {}
-        q_raw = {}
-        og_raw = {}
+        def load(queue, name, src):
+            dst = tile(name, list(src.shape), F32)
+            queue.dma_start(out=dst[:], in_=src)
+            return dst
 
-        def load_k(h, split):
-            if split:
-                for g in range(PASSES):
-                    raw = tile("k_raw%d%d" % (h, g), [P, 512], F32)
-                    nc.sync.dma_start(out=raw[:], in_=k_rows[h, :, g, :])
-                    k_raw[h, g] = raw[:]
-            else:
-                raw = tile("k_raw%d" % h, [P, PASSES, 512], F32)
-                nc.sync.dma_start(out=raw[:], in_=k_rows[h])
-                for g in range(PASSES):
-                    k_raw[h, g] = raw[:, g, :]
+        def mx_tiles(name, count, words):
+            codes = [tile("%s_codes%d" % (name, i), [P, words], U32) for i in range(count)]
+            scales = [tile("%s_scales%d" % (name, i), [P, words], U8) for i in range(count)]
+            return codes, scales
+
+        k_raw, v_raw, q_raw, og_raw = {}, {}, {}, {}
+        q_width = N // Q_LOADS
+
+        def load_k(h, g):
+            k_raw[h, g] = load(nc.sync, "k_raw%d%d" % (h, g), k_rows[h, :, g, :])
 
         def load_v(h):
-            raw = tile("v_raw%d" % h, [P, PASSES, 512], F32)
-            nc.sync.dma_start(out=raw[:], in_=v_rows[h])
-            v_raw[h] = raw
+            v_raw[h] = load(nc.sync, "v_raw%d" % h, v_rows[h])
 
         def load_q(c):
-            raw = tile("q_raw%d" % c, [P, PACK, QW], F32)
-            nc.sync.dma_start(out=raw[:], in_=q_rows[:, :, c * QW : (c + 1) * QW])
-            q_raw[c] = raw
+            q_raw[c] = load(nc.sync, "q_raw%d" % c, q_rows[:, :, c * q_width : (c + 1) * q_width])
 
         def load_og(queue, h, lo, hi):
-            raw = tile("og_raw%d_%d" % (h, lo), [P, hi - lo], F32)
-            queue.dma_start(out=raw[:], in_=og_rows[h, :, lo:hi])
-            og_raw[h, lo] = raw
+            og_raw[h, lo] = load(queue, "og_raw%d_%d" % (h, lo), og_rows[h, :, lo:hi])
 
-        tka = [tile("tka%d" % g, [P, 512], F32) for g in range(PASSES)]
-        k_sq = {}
-        fk = [tile("fk%d" % g, [P, PACK, H, 128], BF16) for g in range(PASSES)]
-        fk_codes = [tile("fk_codes%d" % g, [P, 512], U32) for g in range(PASSES)]
-        fk_scales = [tile("fk_scales%d" % g, [P, 512], U8) for g in range(PASSES)]
-        v_bf = [tile("v_bf%d" % h, [P, PASSES, 128, PACK], BF16) for h in range(H)]
-        v_codes = [tile("v_codes%d" % h, [P, 256], U32) for h in range(H)]
-        v_scales = [tile("v_scales%d" % h, [P, 256], U8) for h in range(H)]
-        q_sq = {}
-        fq = [tile("fq%d" % u, [P, 4, 128, PACK], BF16) for u in range(2)]
-        fq_codes = [tile("fq_codes%d" % u, [P, 512], U32) for u in range(2)]
-        fq_scales = [tile("fq_scales%d" % u, [P, 512], U8) for u in range(2)]
-        state_bf = tile("state_bf", [P, 128, PACK], BF16)
-        state_codes = [tile("state_codes%d" % h, [P, 128], U32) for h in range(H)]
-        state_scales = [tile("state_scales%d" % h, [P, 128], U8) for h in range(H)]
-        gate = {(h, u): tile("gate%d%d" % (h, u), [P, 512], F32) for h in range(H) for u in range(2)}
-        result = [tile("result%d" % h, [P, 1024], F32) for h in range(H)]
-        state_bank = [ps.tile([P, PACK, 128], F32, name="state_bank%d" % i) for i in range(2)]
-        y_banks = [ps.tile([P, 512], F32, name="y_bank%d" % i) for i in range(6)]
-        y_bank = {(0, 0): y_banks[0], (0, 1): y_banks[0], (1, 0): y_banks[1], (1, 1): y_banks[1],
-                  (2, 0): y_banks[2], (2, 1): y_banks[3], (3, 0): y_banks[4], (3, 1): y_banks[5]}
+        load_k(0, 0)
+        ka_sb = load(nc.scalar, "ka_sb", ka)
+        t_sb = load(nc.scalar, "t_sb", t.rearrange("(g p j) o -> p g (j o)", g=PASSES, j=PACK))
+        load_og(nc.scalar, 0, 0, FIRST_GATE)
+        for h in range(1, H):
+            load_k(h, 0)
+        load_k(0, 1)
+        qa_sb = tile("qa_sb", [P, PACK], F32)
+        nc.sync.dma_start(
+            out=qa_sb[:],
+            in_=qa.rearrange("(p j) o -> p (j o)", j=PACK).unsqueeze(0).to_broadcast([H, ROWS, PACK]),
+        )
+        for h in range(1, H):
+            load_k(h, 1)
+        load_v(0)
+        load_q(0)
+        load_v(1)
+        load_q(1)
+        load_v(2)
+        load_v(3)
+        load_og(nc.sync, 0, FIRST_GATE, HALVES * BANK)
+        load_og(nc.sync, 1, 0, HALVES * BANK)
+        load_og(nc.sync, 2, 0, HALVES * BANK)
+        for u in range(HALVES):
+            load_og(nc.sync, 3, u * BANK, (u + 1) * BANK)
 
-        def make_tka(g):
+        key_weight = [tile("key_weight%d" % g, [P, PACK, ROWS, PACK], F32) for g in range(PASSES)]
+        query_weight = tile("query_weight", [P, Q_M, PACK], F32)
+        k_sq, q_sq = {}, {}
+        fk = [tile("fk%d" % g, [P, PACK, H, ROWS * PACK], BF16) for g in range(PASSES)]
+        v_bf = [tile("v_bf%d" % h, [P, PASSES, D, PACK], BF16) for h in range(H)]
+        fq = [tile("fq%d" % u, [P, PACK, P * PACK], BF16) for u in range(HALVES)]
+        state_bf = tile("state_bf", [P, D, PACK], BF16)
+        fk_codes, fk_scales = mx_tiles("fk", PASSES, H * D)
+        v_codes, v_scales = mx_tiles("v", H, PASSES * D)
+        fq_codes, fq_scales = mx_tiles("fq", HALVES, PACK * P)
+        state_call = [0, 0, 1, 2]
+        state_codes, state_scales = mx_tiles("state", 3, D)
+        gate = [tile("gate%d" % h, [P, HALVES * BANK], F32) for h in range(H)]
+        result = [tile("result%d" % h, [P, HALVES * BANK], F32) for h in range(H)]
+        state_bank = [psum.tile([P, PACK, D], F32, name="state_bank%d" % i) for i in range(2)]
+        y_bank = {}
+        for h in range(H):
+            for u in range(HALVES):
+                if h < 2 and u == 1:
+                    y_bank[h, u] = y_bank[h, 0]
+                else:
+                    y_bank[h, u] = psum.tile([P, BANK], F32, name="y_bank%d%d" % (h, u))
+
+        def quantize(codes, scales, values):
+            nc.vector.quantize_mx(out=codes.bitcast(FP8X4), scales=scales, in_=values)
+
+        def make_key_weight(g):
             shape = [P, PACK, ROWS, PACK]
             nc.vector.tensor_tensor(
-                out=tka[g][:].rearrange("p (x m j) -> p x m j", x=PACK, j=PACK),
+                out=key_weight[g][:],
                 in0=ka_sb[:].rearrange("p (m x) -> p x m", x=PACK).unsqueeze(3).to_broadcast(shape),
                 in1=t_sb[:, g, :].unsqueeze(1).unsqueeze(1).to_broadcast(shape),
                 op=ALU.mult,
             )
 
         def square_k(h, g):
-            sq = tile("k_sq%d%d" % (h, g), [P, 512], F32)
+            k_sq[h, g] = tile("k_sq%d%d" % (h, g), [P, PACK, ROWS, PACK], F32)
             nc.scalar.activation(
-                out=sq[:].rearrange("p (x m j) -> p m j x", x=PACK, j=PACK),
-                in_=k_raw[h, g].rearrange("p (j m x) -> p m j x", j=PACK, x=PACK),
+                out=k_sq[h, g][:].rearrange("p x m j -> p m j x"),
+                in_=k_raw[h, g][:].rearrange("p (j m x) -> p m j x", j=PACK, x=PACK),
                 func=ACT.Square,
             )
-            k_sq[h, g] = sq
 
         def weigh_k(h, g):
             nc.vector.scalar_tensor_tensor(
                 out=fk[g][:, :, h, :],
-                in0=k_sq[h, g][:].rearrange("p (x w) -> p x w", x=PACK),
+                in0=k_sq[h, g][:].rearrange("p x m j -> p x (m j)"),
                 scalar=PHI_BIAS,
-                in1=tka[g][:].rearrange("p (x w) -> p x w", x=PACK),
+                in1=key_weight[g][:].rearrange("p x m j -> p x (m j)"),
                 op0=ALU.add,
                 op1=ALU.mult,
             )
 
-        def quantize(codes, scales, values):
-            nc.vector.quantize_mx(out=codes.bitcast(FP8X4), scales=scales, in_=values)
-
         def quantize_k(g):
             quantize(fk_codes[g][:], fk_scales[g][:], fk[g][:].rearrange("p x h w -> p (x h w)"))
 
-        def round_v(h, on_scalar):
-            dst = v_bf[h][:].rearrange("p g (c i) j -> p g c j i", i=4)
-            src = v_raw[h][:].rearrange("p g (j c i) -> p g c j i", j=PACK, i=4)
-            if on_scalar:
-                nc.scalar.copy(out=dst, in_=src)
-            else:
-                nc.vector.tensor_copy(out=dst, in_=src)
+        def round_v(copy, h, first, last):
+            copy(
+                out=v_bf[h][:, first : last + 1].rearrange("p g (c i) j -> p g c j i", i=PACK),
+                in_=v_raw[h][:, first : last + 1].rearrange("p g (j c i) -> p g c j i", j=PACK, i=PACK),
+            )
 
         def quantize_v(h):
             quantize(v_codes[h][:], v_scales[h][:], v_bf[h][:].rearrange("p g e j -> p (g e j)"))
 
         def state_matmuls(h):
             for x in range(PACK):
-                cols = slice(128 * x, 128 * (x + 1))
+                key_cols = slice(x * P, (x + 1) * P)
                 for g in range(PASSES):
-                    vcols = slice(128 * g, 128 * (g + 1))
+                    value_cols = slice(g * D, (g + 1) * D)
                     nc.tensor.matmul_mx(
                         out=state_bank[h % 2][:, x, :],
-                        lhsT=fk_codes[g][:, cols].bitcast(FP8X4),
-                        lhsT_scale=fk_scales[g][:, cols],
-                        rhs=v_codes[h][:, vcols].bitcast(FP8X4),
-                        rhs_scale=v_scales[h][:, vcols],
+                        lhsT=fk_codes[g][:, key_cols].bitcast(FP8X4),
+                        lhsT_scale=fk_scales[g][:, key_cols],
+                        rhs=v_codes[h][:, value_cols].bitcast(FP8X4),
+                        rhs_scale=v_scales[h][:, value_cols],
                         start=(g == 0),
                         stop=(g == PASSES - 1),
                     )
@@ -166,143 +184,126 @@ def tile_rows_lin_sq_gate_kernel(tc, q, qa, ka, k, t, v, og, out):
 
         def quantize_state(h):
             rows = slice(0, ROWS * (h + 1))
-            quantize(state_codes[h][rows], state_scales[h][rows], state_bf[rows].rearrange("p e x -> p (e x)"))
+            call = state_call[h]
+            quantize(state_codes[call][rows], state_scales[call][rows], state_bf[rows].rearrange("p e x -> p (e x)"))
 
         def square_q(c, u):
-            sq = tile("q_sq%d%d" % (c, u), [P, 4, QW // 8, PACK], F32)
+            pieces = Q_PIECES // Q_LOADS
+            raw = q_raw[c // pieces][:].rearrange("p j (s m u r) -> p s u m j r", m=Q_M, u=HALVES, r=PACK)
+            q_sq[c, u] = tile("q_sq%d%d" % (c, u), [P, PACK, Q_M, PACK], F32)
             nc.scalar.activation(
-                out=sq[:].rearrange("p r m j -> p m j r"),
-                in_=q_raw[c][:].rearrange("p j (m u r) -> p u m j r", u=2, r=4)[:, u],
-                func=ACT.Square,
+                out=q_sq[c, u][:].rearrange("p r m j -> p m j r"), in_=raw[:, c % pieces, u], func=ACT.Square
             )
-            q_sq[c, u] = sq
 
         def weigh_q(c, u):
-            m = QW // 8
+            width = Q_M * PACK
             nc.vector.scalar_tensor_tensor(
-                out=fq[u][:].rearrange("p r m j -> p r (m j)")[:, :, c * m * PACK : (c + 1) * m * PACK],
+                out=fq[u][:, :, c * width : (c + 1) * width],
                 in0=q_sq[c, u][:].rearrange("p r m j -> p r (m j)"),
                 scalar=PHI_BIAS,
-                in1=qa_rep[:].rearrange("p m j -> p (m j)").unsqueeze(1).to_broadcast([P, 4, m * PACK]),
+                in1=query_weight[:].rearrange("p m j -> p (m j)").unsqueeze(1).to_broadcast([P, PACK, width]),
                 op0=ALU.add,
                 op1=ALU.mult,
             )
 
         def quantize_q(u):
-            quantize(fq_codes[u][:], fq_scales[u][:], fq[u][:].rearrange("p r m j -> p (r m j)"))
+            quantize(fq_codes[u][:], fq_scales[u][:], fq[u][:].rearrange("p r w -> p (r w)"))
 
         def read_matmuls(h, u):
             rows = slice(ROWS * h, ROWS * (h + 1))
-            for r in range(4):
-                cols = slice(128 * r, 128 * (r + 1))
+            call = state_call[h]
+            for r in range(PACK):
+                cols = slice(r * P, (r + 1) * P)
                 nc.tensor.matmul_mx(
                     out=y_bank[h, u][:, cols],
                     lhsT=fq_codes[u][rows, cols].bitcast(FP8X4),
                     lhsT_scale=fq_scales[u][rows, cols],
-                    rhs=state_codes[h][rows].bitcast(FP8X4),
-                    rhs_scale=state_scales[h][rows],
+                    rhs=state_codes[call][rows].bitcast(FP8X4),
+                    rhs_scale=state_scales[call][rows],
                     start=True,
                     stop=True,
                 )
 
-        def sigmoid(h, lo, hi, base):
-            u = lo // 512
-            nc.scalar.activation(
-                out=gate[h, u][:, lo - 512 * u : hi - 512 * u],
-                in_=og_raw[h, base][:, lo - base : hi - base],
-                func=ACT.Sigmoid,
-            )
+        def sigmoid(h, lo, hi):
+            base = max(start for head, start in og_raw if head == h and start <= lo)
+            nc.scalar.activation(out=gate[h][:, lo:hi], in_=og_raw[h, base][:, lo - base : hi - base], func=ACT.Sigmoid)
 
-        def apply_gate(h, u):
-            nc.vector.tensor_tensor(
-                out=result[h][:, 512 * u : 512 * (u + 1)], in0=y_bank[h, u][:], in1=gate[h, u][:], op=ALU.mult
-            )
+        def sigmoid_half(h, u):
+            sigmoid(h, FIRST_GATE if (h, u) == (0, 0) else u * BANK, (u + 1) * BANK)
 
-        def store(h, lo, hi):
-            nc.sync.dma_start(out=out_rows[h, :, lo:hi], in_=result[h][:, lo:hi])
+        def gate_and_store(h, u):
+            cols = slice(u * BANK, (u + 1) * BANK)
+            nc.vector.tensor_tensor(out=result[h][:, cols], in0=y_bank[h, u][:], in1=gate[h][:, cols], op=ALU.mult)
+            nc.sync.dma_start(out=out_rows[h, :, cols], in_=result[h][:, cols])
 
-
-        load_k(0, True)
-        nc.scalar.dma_start(out=ka_sb[:], in_=ka)
-        nc.scalar.dma_start(out=t_sb[:], in_=t.rearrange("(g p j) o -> p g (j o)", g=PASSES, j=PACK))
-        load_og(nc.scalar, 0, 0, 128)
-        for h in range(1, H):
-            load_k(h, False)
-        nc.sync.dma_start(
-            out=qa_sb[:], in_=qa.rearrange("(p j) o -> p (j o)", j=PACK).unsqueeze(0).to_broadcast([H, ROWS, PACK])
-        )
-        load_v(0)
-        load_q(0)
-        load_v(1)
-        load_v(2)
-        load_q(1)
-        load_v(3)
-        load_og(nc.sync, 0, 128, 1024)
-        load_og(nc.sync, 1, 0, 1024)
-        load_og(nc.sync, 2, 0, 1024)
-        load_og(nc.sync, 3, 0, 512)
-        load_og(nc.sync, 3, 512, 1024)
-
-        sigmoid(0, 0, 128, 0)
+        sigmoid(0, 0, FIRST_GATE)
         for g in range(PASSES):
-            make_tka(g)
-        for h in range(H):
-            for g in range(PASSES):
+            make_key_weight(g)
+        for g in range(PASSES):
+            for h in range(H):
                 square_k(h, g)
                 weigh_k(h, g)
-        round_v(0, True)
-        nc.vector.tensor_copy(out=qa_rep[:], in_=qa_sb[:].unsqueeze(1).to_broadcast([P, QW // 8, PACK]))
-        quantize_k(0)
+                if (h, g) == (0, 1):
+                    nc.vector.tensor_copy(out=query_weight[:], in_=qa_sb[:].unsqueeze(1).to_broadcast([P, Q_M, PACK]))
+                    quantize_k(0)
+        round_v(nc.scalar.copy, 0, 0, 1)
         quantize_k(1)
         quantize_v(0)
         state_matmuls(0)
-        square_q(0, 0)
-        square_q(0, 1)
-        round_v(1, False)
+
+        for u in range(HALVES):
+            for c in (0, 1):
+                square_q(c, u)
+        round_state(0)
         weigh_q(0, 0)
+        round_v(nc.vector.tensor_copy, 1, 0, 1)
+        weigh_q(1, 0)
         quantize_v(1)
         state_matmuls(1)
-        round_state(0)
-        round_v(2, True)
         weigh_q(0, 1)
-        quantize_state(0)
+        weigh_q(1, 1)
+
+        for c in (2, 3):
+            square_q(c, 0)
+        round_state(1)
+        for c in (2, 3):
+            square_q(c, 1)
+        round_v(nc.scalar.copy, 3, 1, 1)
+        weigh_q(2, 0)
+        round_v(nc.vector.tensor_copy, 2, 0, 1)
+        weigh_q(3, 0)
         quantize_v(2)
         state_matmuls(2)
-        round_state(1)
-        quantize_state(1)
-        square_q(1, 0)
-        square_q(1, 1)
-        round_v(3, False)
-        weigh_q(1, 0)
-        quantize_v(3)
-        state_matmuls(3)
         quantize_q(0)
+        quantize_state(1)
         read_matmuls(0, 0)
         read_matmuls(1, 0)
+        round_v(nc.vector.tensor_copy, 3, 0, 0)
+        weigh_q(2, 1)
+        quantize_v(3)
+        state_matmuls(3)
+        weigh_q(3, 1)
+
+        sigmoid_half(0, 0)
         round_state(2)
-        weigh_q(1, 1)
-        quantize_state(2)
-        quantize_q(1)
-        sigmoid(0, 128, 512, 128)
-        sigmoid(1, 0, 512, 0)
+        sigmoid_half(1, 0)
+        sigmoid_half(0, 1)
         round_state(3)
-        sigmoid(0, 512, 1024, 128)
-        sigmoid(1, 512, 1024, 0)
-        read_matmuls(2, 0)
-        read_matmuls(2, 1)
-        apply_gate(0, 0)
+        sigmoid_half(1, 1)
+        gate_and_store(0, 0)
+        quantize_q(1)
         read_matmuls(0, 1)
-        apply_gate(1, 0)
+        gate_and_store(1, 0)
         read_matmuls(1, 1)
+        quantize_state(2)
+        for u in range(HALVES):
+            read_matmuls(2, u)
+        for h in (0, 1):
+            gate_and_store(h, 1)
         quantize_state(3)
-        read_matmuls(3, 0)
-        read_matmuls(3, 1)
-        apply_gate(0, 1)
-        store(0, 0, 1024)
-        apply_gate(1, 1)
-        store(1, 0, 1024)
+        for u in range(HALVES):
+            read_matmuls(3, u)
         for h in (2, 3):
-            for u in range(2):
-                sigmoid(h, 512 * u, 512 * (u + 1), 512 * u if h == 3 else 0)
-                apply_gate(h, u)
-                store(h, 512 * u, 512 * (u + 1))
+            for u in range(HALVES):
+                sigmoid_half(h, u)
+                gate_and_store(h, u)

from contextlib import ExitStack

import concourse.mybir as mybir

H, D, N = 4, 128, 1024
FLOPS = 2 * 2 * H * N * D * D

F32 = mybir.dt.float32
BF16 = mybir.dt.bfloat16
U32 = mybir.dt.uint32
U8 = mybir.dt.uint8
FP8X4 = mybir.dt.float8_e4m3fn_x4
ACT = mybir.ActivationFunctionType
ALU = mybir.AluOpType

P = 128
PACK = 4
ROWS = D // PACK
PASSES = N // (P * PACK)
BANK = 512
HALVES = 2
PHI_BIAS = 0.125
Q_LOADS = 2
Q_PIECES = 4
Q_M = P // Q_PIECES
FIRST_GATE = D


def tile_rows_lin_sq_gate_kernel(tc, q, qa, ka, k, t, v, og, out):
    nc = tc.nc
    k_rows = k.rearrange("h (g p j) d -> h p g (j d)", g=PASSES, j=PACK)
    v_rows = v.rearrange("h (g p j) e -> h p g (j e)", g=PASSES, j=PACK)
    q_rows = q.rearrange("h (p j) n -> (h p) j n", j=PACK)
    og_rows = og.rearrange("h (m s) e -> h m (s e)", m=P)
    out_rows = out.rearrange("h (m s) e -> h m (s e)", m=P)

    with ExitStack() as ctx:
        sbuf = ctx.enter_context(tc.tile_pool(name="sbuf", bufs=1))
        psum = ctx.enter_context(tc.psum_pool(name="psum", bufs=1))
        ctx.enter_context(tc.manual_schedule())

        def tile(name, shape, dtype):
            return sbuf.tile(shape, dtype, name=name, align_bytes=64)

        def load(queue, name, src):
            dst = tile(name, list(src.shape), F32)
            queue.dma_start(out=dst[:], in_=src)
            return dst

        def mx_tiles(name, count, words):
            codes = [tile("%s_codes%d" % (name, i), [P, words], U32) for i in range(count)]
            scales = [tile("%s_scales%d" % (name, i), [P, words], U8) for i in range(count)]
            return codes, scales

        k_raw, v_raw, q_raw, og_raw = {}, {}, {}, {}
        q_width = N // Q_LOADS

        def load_k(h, g):
            k_raw[h, g] = load(nc.sync, "k_raw%d%d" % (h, g), k_rows[h, :, g, :])

        def load_v(h):
            v_raw[h] = load(nc.sync, "v_raw%d" % h, v_rows[h])

        def load_q(c):
            q_raw[c] = load(nc.sync, "q_raw%d" % c, q_rows[:, :, c * q_width : (c + 1) * q_width])

        def load_og(queue, h, lo, hi):
            og_raw[h, lo] = load(queue, "og_raw%d_%d" % (h, lo), og_rows[h, :, lo:hi])

        load_k(0, 0)
        ka_sb = load(nc.scalar, "ka_sb", ka)
        t_sb = load(nc.scalar, "t_sb", t.rearrange("(g p j) o -> p g (j o)", g=PASSES, j=PACK))
        load_og(nc.scalar, 0, 0, FIRST_GATE)
        for h in range(1, H):
            load_k(h, 0)
        load_k(0, 1)
        qa_sb = tile("qa_sb", [P, PACK], F32)
        nc.sync.dma_start(
            out=qa_sb[:],
            in_=qa.rearrange("(p j) o -> p (j o)", j=PACK).unsqueeze(0).to_broadcast([H, ROWS, PACK]),
        )
        for h in range(1, H):
            load_k(h, 1)
        load_v(0)
        load_q(0)
        load_v(1)
        load_q(1)
        load_v(2)
        load_v(3)
        load_og(nc.sync, 0, FIRST_GATE, HALVES * BANK)
        load_og(nc.sync, 1, 0, HALVES * BANK)
        load_og(nc.sync, 2, 0, HALVES * BANK)
        for u in range(HALVES):
            load_og(nc.sync, 3, u * BANK, (u + 1) * BANK)

        key_weight = [tile("key_weight%d" % g, [P, PACK, ROWS, PACK], F32) for g in range(PASSES)]
        query_weight = tile("query_weight", [P, Q_M, PACK], F32)
        k_sq, q_sq = {}, {}
        fk = [tile("fk%d" % g, [P, PACK, H, ROWS * PACK], BF16) for g in range(PASSES)]
        v_bf = [tile("v_bf%d" % h, [P, PASSES, D, PACK], BF16) for h in range(H)]
        fq = [tile("fq%d" % u, [P, PACK, P * PACK], BF16) for u in range(HALVES)]
        state_bf = tile("state_bf", [P, D, PACK], BF16)
        fk_codes, fk_scales = mx_tiles("fk", PASSES, H * D)
        v_codes, v_scales = mx_tiles("v", H, PASSES * D)
        fq_codes, fq_scales = mx_tiles("fq", HALVES, PACK * P)
        state_call = [0, 0, 1, 2]
        state_codes, state_scales = mx_tiles("state", 3, D)
        gate = [tile("gate%d" % h, [P, HALVES * BANK], F32) for h in range(H)]
        result = [tile("result%d" % h, [P, HALVES * BANK], F32) for h in range(H)]
        state_bank = [psum.tile([P, PACK, D], F32, name="state_bank%d" % i) for i in range(2)]
        y_bank = {}
        for h in range(H):
            for u in range(HALVES):
                if h < 2 and u == 1:
                    y_bank[h, u] = y_bank[h, 0]
                else:
                    y_bank[h, u] = psum.tile([P, BANK], F32, name="y_bank%d%d" % (h, u))

        def quantize(codes, scales, values):
            nc.vector.quantize_mx(out=codes.bitcast(FP8X4), scales=scales, in_=values)

        def make_key_weight(g):
            shape = [P, PACK, ROWS, PACK]
            nc.vector.tensor_tensor(
                out=key_weight[g][:],
                in0=ka_sb[:].rearrange("p (m x) -> p x m", x=PACK).unsqueeze(3).to_broadcast(shape),
                in1=t_sb[:, g, :].unsqueeze(1).unsqueeze(1).to_broadcast(shape),
                op=ALU.mult,
            )

        def square_k(h, g):
            k_sq[h, g] = tile("k_sq%d%d" % (h, g), [P, PACK, ROWS, PACK], F32)
            nc.scalar.activation(
                out=k_sq[h, g][:].rearrange("p x m j -> p m j x"),
                in_=k_raw[h, g][:].rearrange("p (j m x) -> p m j x", j=PACK, x=PACK),
                func=ACT.Square,
            )

        def weigh_k(h, g):
            nc.vector.scalar_tensor_tensor(
                out=fk[g][:, :, h, :],
                in0=k_sq[h, g][:].rearrange("p x m j -> p x (m j)"),
                scalar=PHI_BIAS,
                in1=key_weight[g][:].rearrange("p x m j -> p x (m j)"),
                op0=ALU.add,
                op1=ALU.mult,
            )

        def quantize_k(g):
            quantize(fk_codes[g][:], fk_scales[g][:], fk[g][:].rearrange("p x h w -> p (x h w)"))

        def round_v(copy, h, first, last):
            copy(
                out=v_bf[h][:, first : last + 1].rearrange("p g (c i) j -> p g c j i", i=PACK),
                in_=v_raw[h][:, first : last + 1].rearrange("p g (j c i) -> p g c j i", j=PACK, i=PACK),
            )

        def quantize_v(h):
            quantize(v_codes[h][:], v_scales[h][:], v_bf[h][:].rearrange("p g e j -> p (g e j)"))

        def state_matmuls(h):
            for x in range(PACK):
                key_cols = slice(x * P, (x + 1) * P)
                for g in range(PASSES):
                    value_cols = slice(g * D, (g + 1) * D)
                    nc.tensor.matmul_mx(
                        out=state_bank[h % 2][:, x, :],
                        lhsT=fk_codes[g][:, key_cols].bitcast(FP8X4),
                        lhsT_scale=fk_scales[g][:, key_cols],
                        rhs=v_codes[h][:, value_cols].bitcast(FP8X4),
                        rhs_scale=v_scales[h][:, value_cols],
                        start=(g == 0),
                        stop=(g == PASSES - 1),
                    )

        def round_state(h):
            rows = slice(ROWS * h, ROWS * (h + 1))
            nc.scalar.activation(
                out=state_bf[rows],
                in_=state_bank[h % 2][rows].rearrange("p x e -> p e x"),
                func=ACT.Copy,
                scale=1.0 / N,
            )

        def quantize_state(h):
            rows = slice(0, ROWS * (h + 1))
            call = state_call[h]
            quantize(state_codes[call][rows], state_scales[call][rows], state_bf[rows].rearrange("p e x -> p (e x)"))

        def square_q(c, u):
            pieces = Q_PIECES // Q_LOADS
            raw = q_raw[c // pieces][:].rearrange("p j (s m u r) -> p s u m j r", m=Q_M, u=HALVES, r=PACK)
            q_sq[c, u] = tile("q_sq%d%d" % (c, u), [P, PACK, Q_M, PACK], F32)
            nc.scalar.activation(
                out=q_sq[c, u][:].rearrange("p r m j -> p m j r"), in_=raw[:, c % pieces, u], func=ACT.Square
            )

        def weigh_q(c, u):
            width = Q_M * PACK
            nc.vector.scalar_tensor_tensor(
                out=fq[u][:, :, c * width : (c + 1) * width],
                in0=q_sq[c, u][:].rearrange("p r m j -> p r (m j)"),
                scalar=PHI_BIAS,
                in1=query_weight[:].rearrange("p m j -> p (m j)").unsqueeze(1).to_broadcast([P, PACK, width]),
                op0=ALU.add,
                op1=ALU.mult,
            )

        def quantize_q(u):
            quantize(fq_codes[u][:], fq_scales[u][:], fq[u][:].rearrange("p r w -> p (r w)"))

        def read_matmuls(h, u):
            rows = slice(ROWS * h, ROWS * (h + 1))
            call = state_call[h]
            for r in range(PACK):
                cols = slice(r * P, (r + 1) * P)
                nc.tensor.matmul_mx(
                    out=y_bank[h, u][:, cols],
                    lhsT=fq_codes[u][rows, cols].bitcast(FP8X4),
                    lhsT_scale=fq_scales[u][rows, cols],
                    rhs=state_codes[call][rows].bitcast(FP8X4),
                    rhs_scale=state_scales[call][rows],
                    start=True,
                    stop=True,
                )

        def sigmoid(h, lo, hi):
            base = max(start for head, start in og_raw if head == h and start <= lo)
            nc.scalar.activation(out=gate[h][:, lo:hi], in_=og_raw[h, base][:, lo - base : hi - base], func=ACT.Sigmoid)

        def sigmoid_half(h, u):
            sigmoid(h, FIRST_GATE if (h, u) == (0, 0) else u * BANK, (u + 1) * BANK)

        def gate_and_store(h, u):
            cols = slice(u * BANK, (u + 1) * BANK)
            nc.vector.tensor_tensor(out=result[h][:, cols], in0=y_bank[h, u][:], in1=gate[h][:, cols], op=ALU.mult)
            nc.sync.dma_start(out=out_rows[h, :, cols], in_=result[h][:, cols])

        sigmoid(0, 0, FIRST_GATE)
        for g in range(PASSES):
            make_key_weight(g)
        for g in range(PASSES):
            for h in range(H):
                square_k(h, g)
                weigh_k(h, g)
                if (h, g) == (0, 1):
                    nc.vector.tensor_copy(out=query_weight[:], in_=qa_sb[:].unsqueeze(1).to_broadcast([P, Q_M, PACK]))
                    quantize_k(0)
        round_v(nc.scalar.copy, 0, 0, 1)
        quantize_k(1)
        quantize_v(0)
        state_matmuls(0)

        for u in range(HALVES):
            for c in (0, 1):
                square_q(c, u)
        round_state(0)
        weigh_q(0, 0)
        round_v(nc.vector.tensor_copy, 1, 0, 1)
        weigh_q(1, 0)
        quantize_v(1)
        state_matmuls(1)
        weigh_q(0, 1)
        weigh_q(1, 1)

        for c in (2, 3):
            square_q(c, 0)
        round_state(1)
        for c in (2, 3):
            square_q(c, 1)
        round_v(nc.scalar.copy, 3, 1, 1)
        weigh_q(2, 0)
        round_v(nc.vector.tensor_copy, 2, 0, 1)
        weigh_q(3, 0)
        quantize_v(2)
        state_matmuls(2)
        quantize_q(0)
        quantize_state(1)
        read_matmuls(0, 0)
        read_matmuls(1, 0)
        round_v(nc.vector.tensor_copy, 3, 0, 0)
        weigh_q(2, 1)
        quantize_v(3)
        state_matmuls(3)
        weigh_q(3, 1)

        sigmoid_half(0, 0)
        round_state(2)
        sigmoid_half(1, 0)
        sigmoid_half(0, 1)
        round_state(3)
        sigmoid_half(1, 1)
        gate_and_store(0, 0)
        quantize_q(1)
        read_matmuls(0, 1)
        gate_and_store(1, 0)
        read_matmuls(1, 1)
        quantize_state(2)
        for u in range(HALVES):
            read_matmuls(2, u)
        for h in (0, 1):
            gate_and_store(h, 1)
        quantize_state(3)
        for u in range(HALVES):
            read_matmuls(3, u)
        for h in (2, 3):
            for u in range(HALVES):
                sigmoid_half(h, u)
                gate_and_store(h, u)
